import numpy as np
import ml_dtypes


def mxq(x, axis, fmt="e4m3"):
    dtype, down = {"e4m3": (ml_dtypes.float8_e4m3fn, 7), "e5m2": (ml_dtypes.float8_e5m2, 14)}[fmt]
    v = np.moveaxis(np.asarray(x, np.float32).astype(ml_dtypes.bfloat16).astype(np.float64), axis, -1)
    blocks = v.reshape(v.shape[:-1] + (-1, 32))
    amax = np.abs(blocks).max(-1, keepdims=True)
    byte = np.maximum(np.where(amax > 0, np.frexp(amax)[1] - 1 + 127, 0) - down, 1)
    scale = np.exp2(byte - 127.0)
    codes = (blocks / scale).astype(np.float32).astype(dtype).astype(np.float64)
    return np.moveaxis((codes * scale).reshape(v.shape), -1, axis)


WIDE = False


def mx_kscale(k):
    if not WIDE:
        return np.ones(k)
    levels = np.array([30, -30])
    if k % 512:
        return np.exp2(np.random.permutation(np.resize(levels, k // 32))).repeat(32)
    a = np.empty((k // 512, 16))
    for p in range(k // 512):
        a[p, :8] = np.random.permutation(np.resize(levels, 8))
        for g in range(8):
            far = levels[np.abs(levels - a[p, g]) >= 10]
            a[p, g + 8] = far[np.random.randint(len(far))]
    return np.exp2(a.ravel()).repeat(32)


def f64(x):
    return np.asarray(x).astype(np.float64)


E2M1 = np.array([0.0, 0.5, 1.0, 1.5, 2.0, 3.0, 4.0, 6.0, -0.0, -0.5, -1.0, -1.5, -2.0, -3.0, -4.0, -6.0])


def pack_weight(w, fmt):
    k, n = w.shape
    w = f64(np.asarray(w, np.float32).astype(ml_dtypes.bfloat16)).reshape(k // 32, 32, n)
    amax = np.abs(w).max(1)
    if fmt == "e4m3":
        byte = np.frexp(amax)[1] - 1 + 127 - 7
    else:
        mant, ex = np.frexp(amax / 6.0)
        byte = np.where(mant > 0.5, ex, ex - 1) + 127
    byte = np.clip(np.where(amax > 0, byte, 1), 1, 254)
    scaled = (w * np.exp2(127.0 - byte)[:, None, :]).reshape(k, n).astype(np.float32)
    by_word = np.ascontiguousarray(scaled.reshape(k // 512, 128, 4, n).transpose(0, 1, 3, 2))
    if fmt == "e4m3":
        words = by_word.astype(ml_dtypes.float8_e4m3fn).view(np.uint8)
    else:
        c = by_word.astype(ml_dtypes.float4_e2m1fn).view(np.uint8) & 0xF
        words = (c[..., 0::2] | (c[..., 1::2] << 4)).reshape(k // 512, 128, 2 * n)
    return np.ascontiguousarray(words), np.ascontiguousarray(byte.astype(np.uint8).reshape(k // 512, 16, n))


def unpack_weight(words, scales, fmt):
    g, _, n = scales.shape
    words = np.ascontiguousarray(words).reshape(g, 128, n, -1)
    if fmt == "e4m3":
        vals = words.view(ml_dtypes.float8_e4m3fn).astype(np.float64)
    else:
        nib = np.empty((g, 128, n, 4), np.uint8)
        nib[..., 0::2] = words & 0xF
        nib[..., 1::2] = words >> 4
        vals = E2M1[nib]
    vals = vals * np.repeat(np.exp2(scales.astype(np.float64) - 127.0), 8, axis=1)[..., None]
    return vals.transpose(0, 1, 3, 2).reshape(g * 512, n)


def bf(x):
    return np.asarray(x, np.float32).astype(ml_dtypes.bfloat16)


def planes(Y):
    r, m = Y.shape
    b = f64(bf(Y)).reshape(r // 32, 32, m)
    amax = np.abs(b).max(1)
    byte = np.clip(np.where(amax > 0, np.frexp(amax)[1] - 1 + 127 - 7, 1), 1, 254)
    codes = (b * np.exp2(127.0 - byte)[:, None, :]).reshape(r, m).astype(np.float32).astype(ml_dtypes.float8_e4m3fn).view(np.uint8)
    words = codes.reshape(r // 512, 128, 4, m).transpose(0, 1, 3, 2)
    return np.ascontiguousarray(words), np.ascontiguousarray(byte.astype(np.uint8).reshape(r // 512, 16, m))


K, L, T, B, N = 512, 1024, 1024, 512, 512


def setup_inputs():
    n = np.random.standard_normal
    fk = mx_kscale(K)
    fl = mx_kscale(L)
    wap = pack_weight(n((K, N)) * 1 / np.sqrt(K) * fk[:, None], "e4m3")
    wbp = pack_weight(n((K, N)) * 1 / np.sqrt(K) * fk[:, None], "e2m1")
    xqp = pack_weight(n((L, B)) / fl[:, None], "e4m3")
    wqp = pack_weight(n((L, N)) * 1 / np.sqrt(L) * fl[:, None], "e2m1")
    return {
        "xf": (n((K, T))).astype(np.float32),
        "fa": (np.random.uniform(0.5, 2.0, (K, 1)) / fk[:, None]).astype(np.float32),
        "fb": (np.random.uniform(0.5, 2.0, (K, 1)) / fk[:, None]).astype(np.float32),
        "wa_words": wap[0],
        "wa_scales": wap[1],
        "wb_words": wbp[0],
        "wb_scales": wbp[1],
        "xq_words": xqp[0],
        "xq_scales": xqp[1],
        "wq_words": wqp[0],
        "wq_scales": wqp[1],
    }


def reference(xf, fa, fb, wa_words, wa_scales, wb_words, wb_scales, xq_words, xq_scales, wq_words, wq_scales):
    wau = unpack_weight(wa_words, wa_scales, "e4m3")
    wbu = unpack_weight(wb_words, wb_scales, "e2m1")
    xqu = unpack_weight(xq_words, xq_scales, "e4m3")
    wqu = unpack_weight(wq_words, wq_scales, "e2m1")
    u = f64(xf).reshape(K, B, T // B).max(axis=2) * f64(fa)
    v = 0.3 * np.square(f64(xf).reshape(K, B, T // B).sum(axis=2)) * f64(fb)
    uq = mxq(u, 0, "e4m3")
    vq = mxq(v, 0, "e5m2")
    y = wau.T @ uq + wbu.T @ vq + wqu.T @ xqu
    words, scales = planes(y)
    return y, words, scales

@@ -1,0 +1,231 @@
+from contextlib import ExitStack
+
+import concourse.mybir as mybir
+from concourse.masks import make_identity
+
+K, L, T, B, N = 512, 1024, 1024, 512, 512
+FLOPS = 2 * N * B * (2 * K + L)
+
+F32 = mybir.dt.float32
+BF16 = mybir.dt.bfloat16
+I32 = mybir.dt.int32
+U32 = mybir.dt.uint32
+U8 = mybir.dt.uint8
+E4M3 = mybir.dt.float8_e4m3fn_x4
+E5M2 = mybir.dt.float8_e5m2_x4
+E2M1 = mybir.dt.float4_e2m1fn_x4
+ALU = mybir.AluOpType
+ACT = mybir.ActivationFunctionType
+
+P = 128
+PACK = 4
+CHUNK = 128
+CHUNKS = B // CHUNK
+QUADS = 4
+RUN = 4
+
+
+def tile_mix_features_pooled_over_tokens_pl_kernel(
+    tc, xf, fa, fb, wa_words, wa_scales, wb_words, wb_scales, xq_words, xq_scales, wq_words, wq_scales,
+    out_0, out_1, out_2,
+):
+    nc = tc.nc
+    with ExitStack() as ctx:
+        sb = ctx.enter_context(tc.tile_pool(name="sb", bufs=1))
+        ps = ctx.enter_context(tc.psum_pool(name="ps", bufs=1))
+        ctx.enter_context(tc.manual_schedule())
+
+        def per_chunk(pool, label, shape, dtype):
+            if pool is ps:
+                return [pool.tile(shape, dtype, name="%s%d" % (label, c)) for c in range(CHUNKS)]
+            return [pool.tile(shape, dtype, name="%s%d" % (label, c), align_bytes=64) for c in range(CHUNKS)]
+
+        x = per_chunk(sb, "x", [P, PACK, 2 * CHUNK], F32)
+        larger = per_chunk(sb, "larger", [P, PACK, CHUNK], F32)
+        total = per_chunk(sb, "total", [P, PACK, CHUNK], F32)
+        squared = per_chunk(sb, "squared", [P, PACK, CHUNK], F32)
+        u_bf = per_chunk(sb, "u_bf", [P, CHUNK * PACK], BF16)
+        v_bf = per_chunk(sb, "v_bf", [P, CHUNK * PACK], BF16)
+        u_codes = per_chunk(sb, "u_codes", [P, CHUNK], U32)
+        v_codes = per_chunk(sb, "v_codes", [P, CHUNK], U32)
+        u_scales = per_chunk(sb, "u_scales", [P, CHUNK], U8)
+        v_scales = per_chunk(sb, "v_scales", [P, CHUNK], U8)
+        y_t = per_chunk(sb, "y_t", [P, PACK, P], F32)
+        y = per_chunk(sb, "y", [P, PACK, CHUNK], F32)
+        acc = per_chunk(ps, "acc", [CHUNK, N], F32)
+        flipped = per_chunk(ps, "flipped", [P, PACK, CHUNK], F32)
+
+        y_bf = sb.tile([P, B * PACK], BF16, align_bytes=64)
+        y_codes = sb.tile([P, B], U32, align_bytes=64)
+        y_scales = sb.tile([P, B], U8, align_bytes=64)
+        fa_sb = sb.tile([P, PACK], F32)
+        fb_sb = sb.tile([P, PACK], F32)
+        fv_sb = sb.tile([P, PACK], F32)
+        warm = sb.tile([P, 1], F32)
+        ident = sb.tile([P, P], F32)
+        wa_sb = sb.tile([P, N], U32, align_bytes=64)
+        wb_sb = sb.tile([P, 2 * N], U8, align_bytes=64)
+        xq_sb = sb.tile([P, 2, B], U32, align_bytes=64)
+        wq_sb = sb.tile([P, 2, 2 * N], U8, align_bytes=64)
+        planes = sb.tile([P, 6 * N], U8, align_bytes=64)
+        WB, WA, XQ, WQ = 0, N, 2 * N, 4 * N
+
+        def load_x(c):
+            cols = xf[:, 2 * CHUNK * c : 2 * CHUNK * (c + 1)]
+            nc.sync.dma_start(out=x[c][:], in_=cols.rearrange("(p j) t -> p j t", j=PACK))
+
+        def load_scales(queue, at, scales, q):
+            passes = scales.shape[0]
+            dst = planes[32 * q : 32 * q + 4, at : at + passes * N].bitcast(I32)
+            src = scales[:, 4 * q : 4 * q + 4, :].rearrange("z r n -> r z n").bitcast(I32)
+            queue.dma_start(out=dst.rearrange("r (z n) -> r z n", z=passes), in_=src)
+
+        def pool_pairs(c):
+            nc.vector.tensor_tensor(out=total[c][:], in0=x[c][:, :, 0::2], in1=x[c][:, :, 1::2], op=ALU.add)
+            nc.vector.tensor_tensor(out=larger[c][:], in0=x[c][:, :, 0::2], in1=x[c][:, :, 1::2], op=ALU.max)
+
+        def square(c):
+            nc.scalar.activation(out=squared[c][:], in_=total[c][:], func=ACT.Square)
+
+        def scale_and_group(dst, src, factor):
+            nc.vector.tensor_tensor(
+                out=dst[:].rearrange("p (g i j) -> p g j i", i=RUN, j=PACK),
+                in0=src[:].rearrange("p j (g i) -> p g j i", i=RUN),
+                in1=factor[:].unsqueeze(1).unsqueeze(3).to_broadcast([P, CHUNK // RUN, PACK, RUN]),
+                op=ALU.mult,
+            )
+
+        def quantise_inputs(c):
+            scale_and_group(v_bf[c], squared[c], fv_sb)
+            scale_and_group(u_bf[c], larger[c], fa_sb)
+            nc.vector.quantize_mx(out=v_codes[c][:].bitcast(E5M2), scales=v_scales[c][:], in_=v_bf[c][:])
+            nc.vector.quantize_mx(out=u_codes[c][:].bitcast(E4M3), scales=u_scales[c][:], in_=u_bf[c][:])
+
+        def pooled_passes(c, start, stop):
+            nc.tensor.matmul_mx(
+                out=acc[c][:], lhsT=v_codes[c][:].bitcast(E5M2), lhsT_scale=v_scales[c][:],
+                rhs=wb_sb[:].bitcast(E2M1), rhs_scale=planes[:, WB : WB + N], start=start, stop=False,
+            )
+            nc.tensor.matmul_mx(
+                out=acc[c][:], lhsT=u_codes[c][:].bitcast(E4M3), lhsT_scale=u_scales[c][:],
+                rhs=wa_sb[:].bitcast(E4M3), rhs_scale=planes[:, WA : WA + N], start=False, stop=stop,
+            )
+
+        def pair_passes(c, start, stop):
+            for z in range(2):
+                at = XQ + z * B + c * CHUNK
+                nc.tensor.matmul_mx(
+                    out=acc[c][:], lhsT=xq_sb[:, z, c * CHUNK : (c + 1) * CHUNK].bitcast(E4M3),
+                    lhsT_scale=planes[:, at : at + CHUNK],
+                    rhs=wq_sb[:, z, :].bitcast(E2M1), rhs_scale=planes[:, WQ + z * N : WQ + (z + 1) * N],
+                    start=start and z == 0, stop=stop and z == 1,
+                )
+
+        def drain(c):
+            nc.scalar.copy(out=y_t[c][:], in_=acc[c][:].rearrange("b (p r) -> b r p", r=PACK))
+
+        def flip(c):
+            for r in range(PACK):
+                nc.tensor.transpose(flipped[c][:, r, :], y_t[c][:, r, :], ident[:])
+
+        def grouped_y(c):
+            return y_bf[:, c * CHUNK * PACK : (c + 1) * CHUNK * PACK]
+
+        def round_from_psum(c):
+            nc.scalar.copy(
+                out=grouped_y(c).rearrange("p (b r) -> p b r", r=PACK), in_=flipped[c][:].rearrange("p r b -> p b r")
+            )
+
+        def round_from_sbuf(c):
+            nc.vector.tensor_copy(
+                out=grouped_y(c).rearrange("p (g i r) -> p g r i", i=RUN, r=PACK),
+                in_=y[c][:].rearrange("p r (g i) -> p g r i", i=RUN),
+            )
+
+        def store_y(c):
+            nc.scalar.copy(out=y[c][:], in_=flipped[c][:])
+            cols = out_0[:, c * CHUNK : (c + 1) * CHUNK]
+            nc.sync.dma_start(out=cols.rearrange("(p r) b -> p r b", r=PACK), in_=y[c][:])
+
+        def quantise_y(first, count):
+            lo, hi = first * CHUNK, (first + count) * CHUNK
+            nc.vector.quantize_mx(
+                out=y_codes[:, lo:hi].bitcast(E4M3), scales=y_scales[:, lo:hi], in_=y_bf[:, lo * PACK : hi * PACK]
+            )
+
+        def store_codes(lo, hi):
+            dst = out_1[0].rearrange("p b r -> p (b r)").bitcast(I32)
+            nc.sync.dma_start(out=dst[:, lo:hi], in_=y_codes[:, lo:hi].bitcast(I32))
+
+        nc.vector.memset(planes[:].bitcast(I32), 0)
+        nc.vector.memset(warm[:], 0.0)
+        make_identity(nc, ident[:])
+
+        load_x(0)
+        nc.sync.dma_start(out=fb_sb[:], in_=fb.rearrange("(p j) o -> p (j o)", j=PACK))
+        nc.sync.dma_start(out=fa_sb[:], in_=fa.rearrange("(p j) o -> p (j o)", j=PACK))
+        for q in range(QUADS):
+            load_scales(nc.scalar, WB, wb_scales, q)
+        nc.scalar.activation(out=warm[:], in_=warm[:], func=ACT.Square)
+        load_x(1)
+        nc.sync.dma_start(out=wb_sb[:].bitcast(I32), in_=wb_words[0].bitcast(I32))
+        nc.sync.dma_start(out=wa_sb[:].bitcast(I32), in_=wa_words[0].rearrange("p n t -> p (n t)").bitcast(I32))
+        for q in range(QUADS):
+            load_scales(nc.sync, WA, wa_scales, q)
+        nc.sync.dma_start(out=xq_sb[:].bitcast(I32), in_=xq_words.rearrange("z p n t -> p z (n t)").bitcast(I32))
+        nc.sync.dma_start(out=wq_sb[:].bitcast(I32), in_=wq_words.rearrange("z p n -> p z n").bitcast(I32))
+        for q in range(QUADS):
+            load_scales(nc.sync, XQ, xq_scales, q)
+        for q in range(QUADS):
+            load_scales(nc.sync, WQ, wq_scales, q)
+        load_x(2)
+        load_x(3)
+
+        nc.scalar.mul(out=fv_sb[:], in_=fb_sb[:], mul=0.3)
+
+        pool_pairs(0)
+        square(0)
+        quantise_inputs(0)
+        pooled_passes(0, True, False)
+        pair_passes(0, False, True)
+        pool_pairs(1)
+        square(1)
+        quantise_inputs(1)
+        pair_passes(1, True, False)
+        pooled_passes(1, False, True)
+        drain(0)
+        flip(0)
+        pool_pairs(2)
+        square(2)
+        quantise_inputs(2)
+        pair_passes(2, True, False)
+        drain(1)
+        flip(1)
+        pair_passes(3, True, False)
+        pooled_passes(2, False, True)
+        round_from_psum(0)
+        store_y(0)
+        pool_pairs(3)
+        square(3)
+        quantise_inputs(3)
+        drain(2)
+        flip(2)
+        pooled_passes(3, False, True)
+        round_from_psum(1)
+        store_y(1)
+        store_y(2)
+        quantise_y(0, 2)
+        round_from_sbuf(2)
+        drain(3)
+        flip(3)
+        quantise_y(2, 1)
+        store_codes(0, 3 * CHUNK)
+        store_y(3)
+        round_from_sbuf(3)
+        quantise_y(3, 1)
+        store_codes(3 * CHUNK, B)
+        for q in range(QUADS):
+            queue = nc.scalar if q % 2 == 0 else nc.sync
+            queue.dma_start(
+                out=out_2[0, 4 * q : 4 * q + 4, :].bitcast(I32), in_=y_scales[32 * q : 32 * q + 4, :].bitcast(I32)
+            )

@@ -22,7 +22,7 @@ PACK = 4
 CHUNK = 128
 CHUNKS = B // CHUNK
 QUADS = 4
-RUN = 4
+RUN = 2
 
 
 def tile_mix_features_pooled_over_tokens_pl_kernel(
@@ -41,9 +41,9 @@ def tile_mix_features_pooled_over_tokens_pl_kernel(
             return [pool.tile(shape, dtype, name="%s%d" % (label, c), align_bytes=64) for c in range(CHUNKS)]
 
         x = per_chunk(sb, "x", [P, PACK, 2 * CHUNK], F32)
-        larger = per_chunk(sb, "larger", [P, PACK, CHUNK], F32)
-        total = per_chunk(sb, "total", [P, PACK, CHUNK], F32)
-        squared = per_chunk(sb, "squared", [P, PACK, CHUNK], F32)
+        larger = per_chunk(sb, "larger", [P, CHUNK * PACK], F32)
+        total = per_chunk(sb, "total", [P, CHUNK * PACK], F32)
+        squared = per_chunk(sb, "squared", [P, CHUNK * PACK], F32)
         u_bf = per_chunk(sb, "u_bf", [P, CHUNK * PACK], BF16)
         v_bf = per_chunk(sb, "v_bf", [P, CHUNK * PACK], BF16)
         u_codes = per_chunk(sb, "u_codes", [P, CHUNK], U32)
@@ -81,8 +81,12 @@ def tile_mix_features_pooled_over_tokens_pl_kernel(
             queue.dma_start(out=dst.rearrange("r (z n) -> r z n", z=passes), in_=src)
 
         def pool_pairs(c):
-            nc.vector.tensor_tensor(out=total[c][:], in0=x[c][:, :, 0::2], in1=x[c][:, :, 1::2], op=ALU.add)
-            nc.vector.tensor_tensor(out=larger[c][:], in0=x[c][:, :, 0::2], in1=x[c][:, :, 1::2], op=ALU.max)
+            pairs = x[c][:].rearrange("p j (g i e) -> p g j i e", i=RUN, e=2)
+            for dst, op in ((total[c], ALU.add), (larger[c], ALU.max)):
+                nc.vector.tensor_tensor(
+                    out=dst[:].rearrange("p (g j i) -> p g j i", j=PACK, i=RUN),
+                    in0=pairs[:, :, :, :, 0], in1=pairs[:, :, :, :, 1], op=op,
+                )
 
         def square(c):
             nc.scalar.activation(out=squared[c][:], in_=total[c][:], func=ACT.Square)
@@ -90,25 +94,27 @@ def tile_mix_features_pooled_over_tokens_pl_kernel(
         def scale_and_group(dst, src, factor):
             nc.vector.tensor_tensor(
                 out=dst[:].rearrange("p (g i j) -> p g j i", i=RUN, j=PACK),
-                in0=src[:].rearrange("p j (g i) -> p g j i", i=RUN),
+                in0=src[:].rearrange("p (g j i) -> p g j i", j=PACK, i=RUN),
                 in1=factor[:].unsqueeze(1).unsqueeze(3).to_broadcast([P, CHUNK // RUN, PACK, RUN]),
                 op=ALU.mult,
             )
 
-        def quantise_inputs(c):
-            scale_and_group(v_bf[c], squared[c], fv_sb)
+        def scale_inputs(c):
             scale_and_group(u_bf[c], larger[c], fa_sb)
-            nc.vector.quantize_mx(out=v_codes[c][:].bitcast(E5M2), scales=v_scales[c][:], in_=v_bf[c][:])
+            scale_and_group(v_bf[c], squared[c], fv_sb)
+
+        def quantise_inputs(c):
             nc.vector.quantize_mx(out=u_codes[c][:].bitcast(E4M3), scales=u_scales[c][:], in_=u_bf[c][:])
+            nc.vector.quantize_mx(out=v_codes[c][:].bitcast(E5M2), scales=v_scales[c][:], in_=v_bf[c][:])
 
         def pooled_passes(c, start, stop):
             nc.tensor.matmul_mx(
-                out=acc[c][:], lhsT=v_codes[c][:].bitcast(E5M2), lhsT_scale=v_scales[c][:],
-                rhs=wb_sb[:].bitcast(E2M1), rhs_scale=planes[:, WB : WB + N], start=start, stop=False,
+                out=acc[c][:], lhsT=u_codes[c][:].bitcast(E4M3), lhsT_scale=u_scales[c][:],
+                rhs=wa_sb[:].bitcast(E4M3), rhs_scale=planes[:, WA : WA + N], start=start, stop=False,
             )
             nc.tensor.matmul_mx(
-                out=acc[c][:], lhsT=u_codes[c][:].bitcast(E4M3), lhsT_scale=u_scales[c][:],
-                rhs=wa_sb[:].bitcast(E4M3), rhs_scale=planes[:, WA : WA + N], start=False, stop=stop,
+                out=acc[c][:], lhsT=v_codes[c][:].bitcast(E5M2), lhsT_scale=v_scales[c][:],
+                rhs=wb_sb[:].bitcast(E2M1), rhs_scale=planes[:, WB : WB + N], start=False, stop=stop,
             )
 
         def pair_passes(c, start, stop):
@@ -138,8 +144,8 @@ def tile_mix_features_pooled_over_tokens_pl_kernel(
 
         def round_from_sbuf(c):
             nc.vector.tensor_copy(
-                out=grouped_y(c).rearrange("p (g i r) -> p g r i", i=RUN, r=PACK),
-                in_=y[c][:].rearrange("p r (g i) -> p g r i", i=RUN),
+                out=grouped_y(c).rearrange("p (g i r) -> p g r i", i=2, r=PACK),
+                in_=y[c][:].rearrange("p r (g i) -> p g r i", i=2),
             )
 
         def store_y(c):
@@ -157,69 +163,71 @@ def tile_mix_features_pooled_over_tokens_pl_kernel(
             dst = out_1[0].rearrange("p b r -> p (b r)").bitcast(I32)
             nc.sync.dma_start(out=dst[:, lo:hi], in_=y_codes[:, lo:hi].bitcast(I32))
 
+        def load_words(dst, src):
+            nc.sync.dma_start(out=dst.bitcast(I32), in_=src.bitcast(I32))
+
         nc.vector.memset(planes[:].bitcast(I32), 0)
         nc.vector.memset(warm[:], 0.0)
+        nc.scalar.activation(out=warm[:], in_=warm[:], func=ACT.Square)
         make_identity(nc, ident[:])
+        for q in range(QUADS):
+            load_scales(nc.gpsimd, WQ, wq_scales, q)
 
         load_x(0)
         nc.sync.dma_start(out=fb_sb[:], in_=fb.rearrange("(p j) o -> p (j o)", j=PACK))
         nc.sync.dma_start(out=fa_sb[:], in_=fa.rearrange("(p j) o -> p (j o)", j=PACK))
-        for q in range(QUADS):
-            load_scales(nc.scalar, WB, wb_scales, q)
-        nc.scalar.activation(out=warm[:], in_=warm[:], func=ACT.Square)
-        load_x(1)
-        nc.sync.dma_start(out=wb_sb[:].bitcast(I32), in_=wb_words[0].bitcast(I32))
-        nc.sync.dma_start(out=wa_sb[:].bitcast(I32), in_=wa_words[0].rearrange("p n t -> p (n t)").bitcast(I32))
-        for q in range(QUADS):
-            load_scales(nc.sync, WA, wa_scales, q)
-        nc.sync.dma_start(out=xq_sb[:].bitcast(I32), in_=xq_words.rearrange("z p n t -> p z (n t)").bitcast(I32))
-        nc.sync.dma_start(out=wq_sb[:].bitcast(I32), in_=wq_words.rearrange("z p n -> p z n").bitcast(I32))
-        for q in range(QUADS):
+        for q in (0, 1):
             load_scales(nc.sync, XQ, xq_scales, q)
-        for q in range(QUADS):
-            load_scales(nc.sync, WQ, wq_scales, q)
+        load_x(1)
+        load_words(xq_sb[:], xq_words.rearrange("z p n t -> p z (n t)"))
+        load_words(wq_sb[:], wq_words.rearrange("z p n -> p z n"))
+        for q in (2, 3):
+            load_scales(nc.sync, XQ, xq_scales, q)
+        load_scales(nc.sync, WA, wa_scales, 0)
+        load_words(wa_sb[:], wa_words[0].rearrange("p n t -> p (n t)"))
+        load_words(wb_sb[:], wb_words[0])
         load_x(2)
+        for q in (1, 2, 3):
+            load_scales(nc.sync, WA, wa_scales, q)
+        for q in range(QUADS):
+            load_scales(nc.sync, WB, wb_scales, q)
         load_x(3)
 
         nc.scalar.mul(out=fv_sb[:], in_=fb_sb[:], mul=0.3)
 
-        pool_pairs(0)
-        square(0)
-        quantise_inputs(0)
-        pooled_passes(0, True, False)
-        pair_passes(0, False, True)
-        pool_pairs(1)
-        square(1)
-        quantise_inputs(1)
-        pair_passes(1, True, False)
+        for c in range(CHUNKS):
+            pair_passes(c, True, False)
+        for c in (0, 1, 2):
+            pool_pairs(c)
+            square(c)
+            if c > 0:
+                quantise_inputs(c - 1)
+            scale_inputs(c)
+        pooled_passes(0, False, True)
         pooled_passes(1, False, True)
         drain(0)
-        flip(0)
-        pool_pairs(2)
-        square(2)
-        quantise_inputs(2)
-        pair_passes(2, True, False)
         drain(1)
+        flip(0)
         flip(1)
-        pair_passes(3, True, False)
-        pooled_passes(2, False, True)
-        round_from_psum(0)
-        store_y(0)
         pool_pairs(3)
         square(3)
+        quantise_inputs(2)
+        scale_inputs(3)
         quantise_inputs(3)
+        pooled_passes(2, False, True)
+        store_y(0)
         drain(2)
         flip(2)
         pooled_passes(3, False, True)
-        round_from_psum(1)
         store_y(1)
         store_y(2)
+        for c in (0, 1, 2):
+            round_from_sbuf(c)
         quantise_y(0, 2)
-        round_from_sbuf(2)
-        drain(3)
-        flip(3)
         quantise_y(2, 1)
         store_codes(0, 3 * CHUNK)
+        drain(3)
+        flip(3)
         store_y(3)
         round_from_sbuf(3)
         quantise_y(3, 1)

@@ -41,6 +41,8 @@ def tile_mix_features_pooled_over_tokens_pl_kernel(
             return [pool.tile(shape, dtype, name="%s%d" % (label, c), align_bytes=64) for c in range(CHUNKS)]
 
         x = per_chunk(sb, "x", [P, PACK, 2 * CHUNK], F32)
+        x_first = [sb.tile([P, PACK, CHUNK], F32, name="x_first%d" % h) for h in range(2)]
+        v_rows = [sb.tile([P, PACK, CHUNK], BF16, name="v_rows%d" % c, align_bytes=64) for c in range(2)]
         larger = per_chunk(sb, "larger", [P, CHUNK * PACK], F32)
         total = per_chunk(sb, "total", [P, CHUNK * PACK], F32)
         squared = per_chunk(sb, "squared", [P, CHUNK * PACK], F32)
@@ -51,7 +53,8 @@ def tile_mix_features_pooled_over_tokens_pl_kernel(
         u_scales = per_chunk(sb, "u_scales", [P, CHUNK], U8)
         v_scales = per_chunk(sb, "v_scales", [P, CHUNK], U8)
         y_t = per_chunk(sb, "y_t", [P, PACK, P], F32)
-        y = per_chunk(sb, "y", [P, PACK, CHUNK], F32)
+        y_pair = [sb.tile([P, PACK, 2 * CHUNK], F32, name="y_pair%d" % h) for h in range(2)]
+        y = [y_pair[c // 2][:, :, (c % 2) * CHUNK : (c % 2 + 1) * CHUNK] for c in range(CHUNKS)]
         acc = per_chunk(ps, "acc", [CHUNK, N], F32)
         flipped = per_chunk(ps, "flipped", [P, PACK, CHUNK], F32)
 
@@ -80,13 +83,42 @@ def tile_mix_features_pooled_over_tokens_pl_kernel(
             src = scales[:, 4 * q : 4 * q + 4, :].rearrange("z r n -> r z n").bitcast(I32)
             queue.dma_start(out=dst.rearrange("r (z n) -> r z n", z=passes), in_=src)
 
+        def load_x_first(h):
+            cols = xf[:, CHUNK * h : CHUNK * (h + 1)]
+            nc.sync.dma_start(out=x_first[h][:], in_=cols.rearrange("(p j) t -> p j t", j=PACK))
+
+        def pool(src, dst, op):
+            pairs = src.rearrange("p j (g i e) -> p g j i e", i=RUN, e=2)
+            nc.vector.tensor_tensor(
+                out=dst.rearrange("p (g j i) -> p g j i", j=PACK, i=RUN),
+                in0=pairs[:, :, :, :, 0], in1=pairs[:, :, :, :, 1], op=op,
+            )
+
         def pool_pairs(c):
-            pairs = x[c][:].rearrange("p j (g i e) -> p g j i e", i=RUN, e=2)
-            for dst, op in ((total[c], ALU.add), (larger[c], ALU.max)):
-                nc.vector.tensor_tensor(
-                    out=dst[:].rearrange("p (g j i) -> p g j i", j=PACK, i=RUN),
-                    in0=pairs[:, :, :, :, 0], in1=pairs[:, :, :, :, 1], op=op,
+            pool(x[c][:], total[c][:], ALU.add)
+            pool(x[c][:], larger[c][:], ALU.max)
+
+        def pool_first():
+            half = CHUNK * PACK // 2
+            for h in range(2):
+                pool(x_first[h][:], total[0][:, h * half : (h + 1) * half], ALU.add)
+                pool(x_first[h][:], larger[0][:, h * half : (h + 1) * half], ALU.max)
+
+        def v_on_scalar(c):
+            by_row = squared[c][:].rearrange("p (j g i) -> p j g i", j=PACK, i=RUN)
+            nc.scalar.activation(
+                out=by_row.rearrange("p j g i -> p g j i"),
+                in_=total[c][:].rearrange("p (g j i) -> p g j i", j=PACK, i=RUN), func=ACT.Square,
+            )
+            for j in range(PACK):
+                nc.scalar.activation(
+                    out=v_rows[c][:, j, :], in_=squared[c][:, j * CHUNK : (j + 1) * CHUNK], func=ACT.Copy,
+                    scale=fv_sb[:, j : j + 1],
                 )
+            nc.scalar.copy(
+                out=v_bf[c][:].rearrange("p (g i j) -> p g j i", i=4, j=PACK),
+                in_=v_rows[c][:].rearrange("p j (g i) -> p g j i", i=4),
+            )
 
         def square(c):
             nc.scalar.activation(out=squared[c][:], in_=total[c][:], func=ACT.Square)
@@ -104,17 +136,17 @@ def tile_mix_features_pooled_over_tokens_pl_kernel(
             scale_and_group(v_bf[c], squared[c], fv_sb)
 
         def quantise_inputs(c):
-            nc.vector.quantize_mx(out=u_codes[c][:].bitcast(E4M3), scales=u_scales[c][:], in_=u_bf[c][:])
             nc.vector.quantize_mx(out=v_codes[c][:].bitcast(E5M2), scales=v_scales[c][:], in_=v_bf[c][:])
+            nc.vector.quantize_mx(out=u_codes[c][:].bitcast(E4M3), scales=u_scales[c][:], in_=u_bf[c][:])
 
         def pooled_passes(c, start, stop):
             nc.tensor.matmul_mx(
-                out=acc[c][:], lhsT=u_codes[c][:].bitcast(E4M3), lhsT_scale=u_scales[c][:],
-                rhs=wa_sb[:].bitcast(E4M3), rhs_scale=planes[:, WA : WA + N], start=start, stop=False,
+                out=acc[c][:], lhsT=v_codes[c][:].bitcast(E5M2), lhsT_scale=v_scales[c][:],
+                rhs=wb_sb[:].bitcast(E2M1), rhs_scale=planes[:, WB : WB + N], start=start, stop=False,
             )
             nc.tensor.matmul_mx(
-                out=acc[c][:], lhsT=v_codes[c][:].bitcast(E5M2), lhsT_scale=v_scales[c][:],
-                rhs=wb_sb[:].bitcast(E2M1), rhs_scale=planes[:, WB : WB + N], start=False, stop=stop,
+                out=acc[c][:], lhsT=u_codes[c][:].bitcast(E4M3), lhsT_scale=u_scales[c][:],
+                rhs=wa_sb[:].bitcast(E4M3), rhs_scale=planes[:, WA : WA + N], start=False, stop=stop,
             )
 
         def pair_passes(c, start, stop):
@@ -129,6 +161,35 @@ def tile_mix_features_pooled_over_tokens_pl_kernel(
 
         def drain(c):
             nc.scalar.copy(out=y_t[c][:], in_=acc[c][:].rearrange("b (p r) -> b r p", r=PACK))
+
+        def finish_last(c):
+            banks = (flipped[c], flipped[0])
+            for h in range(2):
+                rows = slice(2 * h, 2 * h + 2)
+                nc.scalar.copy(out=y_t[c][:, rows, :], in_=acc[c][:].rearrange("b (p r) -> b r p", r=PACK)[:, rows, :])
+            for h in range(2):
+                for r in range(2):
+                    nc.tensor.transpose(banks[h][:, r, :], y_t[c][:, 2 * h + r, :], ident[:])
+            nc.vector.tensor_copy(out=y[c][:, 0:2, :], in_=banks[0][:, 0:2, :])
+            nc.scalar.copy(out=y[c][:, 2:4, :], in_=banks[1][:, 0:2, :])
+            cols = out_0[:, c * CHUNK : (c + 1) * CHUNK]
+            nc.sync.dma_start(out=cols.rearrange("(p r) b -> p r b", r=PACK), in_=y[c][:])
+
+        def drain_half(c, h):
+            rows = slice(2 * h, 2 * h + 2)
+            nc.scalar.copy(out=y_t[c][:, rows, :], in_=acc[c][:].rearrange("b (p r) -> b r p", r=PACK)[:, rows, :])
+
+        def flip_half(c, h):
+            for r in range(2):
+                nc.tensor.transpose((flipped[c], flipped[0])[h][:, r, :], y_t[c][:, 2 * h + r, :], ident[:])
+
+        def store_pair(h):
+            cols = out_0[:, 2 * h * CHUNK : 2 * (h + 1) * CHUNK]
+            nc.sync.dma_start(out=cols.rearrange("(p r) b -> p r b", r=PACK), in_=y_pair[h][:])
+
+        def store_out(c):
+            cols = out_0[:, c * CHUNK : (c + 1) * CHUNK]
+            nc.sync.dma_start(out=cols.rearrange("(p r) b -> p r b", r=PACK), in_=y[c][:])
 
         def flip(c):
             for r in range(PACK):
@@ -153,6 +214,11 @@ def tile_mix_features_pooled_over_tokens_pl_kernel(
             cols = out_0[:, c * CHUNK : (c + 1) * CHUNK]
             nc.sync.dma_start(out=cols.rearrange("(p r) b -> p r b", r=PACK), in_=y[c][:])
 
+        def store_y_vector(c):
+            nc.vector.tensor_copy(out=y[c][:], in_=flipped[c][:])
+            cols = out_0[:, c * CHUNK : (c + 1) * CHUNK]
+            nc.sync.dma_start(out=cols.rearrange("(p r) b -> p r b", r=PACK), in_=y[c][:])
+
         def quantise_y(first, count):
             lo, hi = first * CHUNK, (first + count) * CHUNK
             nc.vector.quantize_mx(
@@ -170,68 +236,91 @@ def tile_mix_features_pooled_over_tokens_pl_kernel(
         nc.vector.memset(warm[:], 0.0)
         nc.scalar.activation(out=warm[:], in_=warm[:], func=ACT.Square)
         make_identity(nc, ident[:])
-        for q in range(QUADS):
-            load_scales(nc.gpsimd, WQ, wq_scales, q)
+        load_scales(nc.gpsimd, WQ, wq_scales, 0)
+        load_scales(nc.gpsimd, WQ, wq_scales, 1)
+        load_scales(nc.gpsimd, WQ, wq_scales, 2)
+        load_scales(nc.gpsimd, WQ, wq_scales, 3)
 
         load_x(0)
         nc.sync.dma_start(out=fb_sb[:], in_=fb.rearrange("(p j) o -> p (j o)", j=PACK))
         nc.sync.dma_start(out=fa_sb[:], in_=fa.rearrange("(p j) o -> p (j o)", j=PACK))
-        for q in (0, 1):
-            load_scales(nc.sync, XQ, xq_scales, q)
+        load_scales(nc.sync, XQ, xq_scales, 0)
+        load_scales(nc.sync, XQ, xq_scales, 1)
         load_x(1)
         load_words(xq_sb[:], xq_words.rearrange("z p n t -> p z (n t)"))
-        load_words(wq_sb[:], wq_words.rearrange("z p n -> p z n"))
-        for q in (2, 3):
-            load_scales(nc.sync, XQ, xq_scales, q)
-        load_scales(nc.sync, WA, wa_scales, 0)
-        load_words(wa_sb[:], wa_words[0].rearrange("p n t -> p (n t)"))
-        load_words(wb_sb[:], wb_words[0])
         load_x(2)
-        for q in (1, 2, 3):
-            load_scales(nc.sync, WA, wa_scales, q)
-        for q in range(QUADS):
-            load_scales(nc.sync, WB, wb_scales, q)
+        load_scales(nc.sync, XQ, xq_scales, 2)
+        load_scales(nc.sync, XQ, xq_scales, 3)
+        load_scales(nc.sync, WB, wb_scales, 0)
+        load_scales(nc.sync, WB, wb_scales, 1)
+        load_words(wq_sb[:], wq_words.rearrange("z p n -> p z n"))
+        load_words(wb_sb[:], wb_words[0])
         load_x(3)
+        load_words(wa_sb[:], wa_words[0].rearrange("p n t -> p (n t)"))
+        load_scales(nc.sync, WB, wb_scales, 2)
+        load_scales(nc.sync, WB, wb_scales, 3)
+        load_scales(nc.sync, WA, wa_scales, 0)
+        load_scales(nc.sync, WA, wa_scales, 1)
+        load_scales(nc.sync, WA, wa_scales, 2)
+        load_scales(nc.sync, WA, wa_scales, 3)
 
         nc.scalar.mul(out=fv_sb[:], in_=fb_sb[:], mul=0.3)
 
-        for c in range(CHUNKS):
-            pair_passes(c, True, False)
-        for c in (0, 1, 2):
-            pool_pairs(c)
-            square(c)
-            if c > 0:
-                quantise_inputs(c - 1)
-            scale_inputs(c)
+        pool(x[0][:], total[0][:], ALU.add)
+        v_on_scalar(0)
+        pool(x[0][:], larger[0][:], ALU.max)
+        scale_and_group(u_bf[0], larger[0], fa_sb)
+        pool(x[1][:], total[1][:], ALU.add)
+        v_on_scalar(1)
+        pool(x[1][:], larger[1][:], ALU.max)
+        scale_and_group(u_bf[1], larger[1], fa_sb)
+        quantise_inputs(0)
+        pool(x[2][:], total[2][:], ALU.add)
+        square(2)
+        pool(x[2][:], larger[2][:], ALU.max)
+        quantise_inputs(1)
+        scale_and_group(u_bf[2], larger[2], fa_sb)
+        scale_and_group(v_bf[2], squared[2], fv_sb)
+        pair_passes(0, True, False)
+        pair_passes(1, True, False)
+        pair_passes(2, True, False)
+        pool(x[3][:], total[3][:], ALU.add)
+        square(3)
         pooled_passes(0, False, True)
         pooled_passes(1, False, True)
         drain(0)
+        quantise_inputs(2)
+        pool(x[3][:], larger[3][:], ALU.max)
+        scale_and_group(v_bf[3], squared[3], fv_sb)
+        scale_and_group(u_bf[3], larger[3], fa_sb)
+        quantise_inputs(3)
         drain(1)
+        pair_passes(3, True, False)
+        pooled_passes(2, False, True)
         flip(0)
         flip(1)
-        pool_pairs(3)
-        square(3)
-        quantise_inputs(2)
-        scale_inputs(3)
-        quantise_inputs(3)
-        pooled_passes(2, False, True)
-        store_y(0)
         drain(2)
-        flip(2)
+        nc.scalar.copy(out=y[0][:], in_=flipped[0][:])
         pooled_passes(3, False, True)
-        store_y(1)
-        store_y(2)
-        for c in (0, 1, 2):
-            round_from_sbuf(c)
+        flip(2)
+        nc.vector.tensor_copy(out=y[1][:], in_=flipped[1][:])
+        store_pair(0)
+        drain_half(3, 0)
+        drain_half(3, 1)
+        round_from_sbuf(0)
+        round_from_sbuf(1)
         quantise_y(0, 2)
-        quantise_y(2, 1)
-        store_codes(0, 3 * CHUNK)
-        drain(3)
-        flip(3)
-        store_y(3)
+        store_codes(0, 2 * CHUNK)
+        nc.scalar.copy(out=y[2][:], in_=flipped[2][:])
+        flip_half(3, 0)
+        flip_half(3, 1)
+        nc.vector.tensor_copy(out=y[3][:, 0:2, :], in_=flipped[3][:, 0:2, :])
+        nc.scalar.copy(out=y[3][:, 2:4, :], in_=flipped[0][:, 0:2, :])
+        store_pair(1)
+        round_from_sbuf(2)
         round_from_sbuf(3)
-        quantise_y(3, 1)
-        store_codes(3 * CHUNK, B)
+        quantise_y(2, 2)
+        store_codes(2 * CHUNK, B)
         for q in range(QUADS):
             queue = nc.scalar if q % 2 == 0 else nc.sync
             queue.dma_start(

@@ -3,7 +3,7 @@ from contextlib import ExitStack
 import concourse.mybir as mybir
 from concourse.masks import make_identity
 
-K, L, T, B, N = 512, 1024, 1024, 512, 512
+K, L, B, N = 512, 1024, 512, 512
 FLOPS = 2 * N * B * (2 * K + L)
 
 F32 = mybir.dt.float32
@@ -19,10 +19,15 @@ ACT = mybir.ActivationFunctionType
 
 P = 128
 PACK = 4
+QUADS = 4
+L_PASSES = L // (P * PACK)
 CHUNK = 128
 CHUNKS = B // CHUNK
-QUADS = 4
+LAST = CHUNKS - 1
+MX_ALIGN = 64
 RUN = 2
+RUN_BF = 4
+WB_AT, WA_AT, XQ_AT, WQ_AT, PLANE_COLS = 0, N, 2 * N, 4 * N, 6 * N
 
 
 def tile_mix_features_pooled_over_tokens_pl_kernel(
@@ -35,80 +40,73 @@ def tile_mix_features_pooled_over_tokens_pl_kernel(
         ps = ctx.enter_context(tc.psum_pool(name="ps", bufs=1))
         ctx.enter_context(tc.manual_schedule())
 
-        def per_chunk(pool, label, shape, dtype):
-            if pool is ps:
-                return [pool.tile(shape, dtype, name="%s%d" % (label, c)) for c in range(CHUNKS)]
-            return [pool.tile(shape, dtype, name="%s%d" % (label, c), align_bytes=64) for c in range(CHUNKS)]
+        def per_chunk(label, shape, dtype, count=CHUNKS):
+            return [sb.tile(shape, dtype, name="%s%d" % (label, c), align_bytes=MX_ALIGN) for c in range(count)]
 
-        x = per_chunk(sb, "x", [P, PACK, 2 * CHUNK], F32)
-        x_first = [sb.tile([P, PACK, CHUNK], F32, name="x_first%d" % h) for h in range(2)]
-        v_rows = [sb.tile([P, PACK, CHUNK], BF16, name="v_rows%d" % c, align_bytes=64) for c in range(2)]
-        larger = per_chunk(sb, "larger", [P, CHUNK * PACK], F32)
-        total = per_chunk(sb, "total", [P, CHUNK * PACK], F32)
-        squared = per_chunk(sb, "squared", [P, CHUNK * PACK], F32)
-        u_bf = per_chunk(sb, "u_bf", [P, CHUNK * PACK], BF16)
-        v_bf = per_chunk(sb, "v_bf", [P, CHUNK * PACK], BF16)
-        u_codes = per_chunk(sb, "u_codes", [P, CHUNK], U32)
-        v_codes = per_chunk(sb, "v_codes", [P, CHUNK], U32)
-        u_scales = per_chunk(sb, "u_scales", [P, CHUNK], U8)
-        v_scales = per_chunk(sb, "v_scales", [P, CHUNK], U8)
-        y_t = per_chunk(sb, "y_t", [P, PACK, P], F32)
-        y_pair = [sb.tile([P, PACK, 2 * CHUNK], F32, name="y_pair%d" % h) for h in range(2)]
-        y = [y_pair[c // 2][:, :, (c % 2) * CHUNK : (c % 2 + 1) * CHUNK] for c in range(CHUNKS)]
-        acc = per_chunk(ps, "acc", [CHUNK, N], F32)
-        flipped = per_chunk(ps, "flipped", [P, PACK, CHUNK], F32)
+        x = per_chunk("x", [P, PACK, 2 * CHUNK], F32)
+        larger = per_chunk("larger", [P, CHUNK * PACK], F32)
+        total = per_chunk("total", [P, CHUNK * PACK], F32)
+        squared = per_chunk("squared", [P, CHUNK * PACK], F32)
+        v_rows = per_chunk("v_rows", [P, PACK, CHUNK], BF16, LAST)
+        u_bf = per_chunk("u_bf", [P, CHUNK * PACK], BF16)
+        v_bf = per_chunk("v_bf", [P, CHUNK * PACK], BF16)
+        u_codes = per_chunk("u_codes", [P, CHUNK], U32)
+        v_codes = per_chunk("v_codes", [P, CHUNK], U32)
+        u_scales = per_chunk("u_scales", [P, CHUNK], U8)
+        v_scales = per_chunk("v_scales", [P, CHUNK], U8)
+        y_t = per_chunk("y_t", [CHUNK, PACK, P], F32)
+        y_two = per_chunk("y_two", [P, PACK, 2 * CHUNK], F32, CHUNKS // 2)
+        y = [y_two[c // 2][:, :, (c % 2) * CHUNK : (c % 2 + 1) * CHUNK] for c in range(CHUNKS)]
+        acc = [ps.tile([CHUNK, N], F32, name="acc%d" % c) for c in range(CHUNKS)]
+        flipped = [ps.tile([P, PACK, CHUNK], F32, name="flipped%d" % c) for c in range(CHUNKS)]
 
-        y_bf = sb.tile([P, B * PACK], BF16, align_bytes=64)
-        y_codes = sb.tile([P, B], U32, align_bytes=64)
-        y_scales = sb.tile([P, B], U8, align_bytes=64)
+        y_bf = sb.tile([P, B * PACK], BF16, align_bytes=MX_ALIGN)
+        y_codes = sb.tile([P, B], U32, align_bytes=MX_ALIGN)
+        y_scales = sb.tile([P, B], U8, align_bytes=MX_ALIGN)
         fa_sb = sb.tile([P, PACK], F32)
         fb_sb = sb.tile([P, PACK], F32)
         fv_sb = sb.tile([P, PACK], F32)
         warm = sb.tile([P, 1], F32)
         ident = sb.tile([P, P], F32)
-        wa_sb = sb.tile([P, N], U32, align_bytes=64)
-        wb_sb = sb.tile([P, 2 * N], U8, align_bytes=64)
-        xq_sb = sb.tile([P, 2, B], U32, align_bytes=64)
-        wq_sb = sb.tile([P, 2, 2 * N], U8, align_bytes=64)
-        planes = sb.tile([P, 6 * N], U8, align_bytes=64)
-        WB, WA, XQ, WQ = 0, N, 2 * N, 4 * N
+        wa_sb = sb.tile([P, N], U32, align_bytes=MX_ALIGN)
+        wb_sb = sb.tile([P, 2 * N], U8, align_bytes=MX_ALIGN)
+        xq_sb = sb.tile([P, L_PASSES, B], U32, align_bytes=MX_ALIGN)
+        wq_sb = sb.tile([P, L_PASSES, 2 * N], U8, align_bytes=MX_ALIGN)
+        planes = sb.tile([P, PLANE_COLS], U8, align_bytes=MX_ALIGN)
 
         def load_x(c):
             cols = xf[:, 2 * CHUNK * c : 2 * CHUNK * (c + 1)]
             nc.sync.dma_start(out=x[c][:], in_=cols.rearrange("(p j) t -> p j t", j=PACK))
 
-        def load_scales(queue, at, scales, q):
+        def load_words(dst, src):
+            nc.sync.dma_start(out=dst.bitcast(I32), in_=src.bitcast(I32))
+
+        def load_scales(queue, at, scales):
             passes = scales.shape[0]
-            dst = planes[32 * q : 32 * q + 4, at : at + passes * N].bitcast(I32)
-            src = scales[:, 4 * q : 4 * q + 4, :].rearrange("z r n -> r z n").bitcast(I32)
-            queue.dma_start(out=dst.rearrange("r (z n) -> r z n", z=passes), in_=src)
+            for q in range(QUADS):
+                dst = planes[32 * q : 32 * q + 4, at : at + passes * N].bitcast(I32)
+                src = scales[:, 4 * q : 4 * q + 4, :].rearrange("z r n -> r z n").bitcast(I32)
+                queue.dma_start(out=dst.rearrange("r (z n) -> r z n", z=passes), in_=src)
 
-        def load_x_first(h):
-            cols = xf[:, CHUNK * h : CHUNK * (h + 1)]
-            nc.sync.dma_start(out=x_first[h][:], in_=cols.rearrange("(p j) t -> p j t", j=PACK))
+        def by_run(tile):
+            return tile[:].rearrange("p (g j i) -> p g j i", j=PACK, i=RUN)
 
-        def pool(src, dst, op):
-            pairs = src.rearrange("p j (g i e) -> p g j i e", i=RUN, e=2)
+        def pool_pairs(c, dst, op):
+            pairs = x[c][:].rearrange("p j (g i e) -> p g j i e", i=RUN, e=2)
+            nc.vector.tensor_tensor(out=by_run(dst), in0=pairs[:, :, :, :, 0], in1=pairs[:, :, :, :, 1], op=op)
+
+        def scale_on_vector(dst, src, factor):
             nc.vector.tensor_tensor(
-                out=dst.rearrange("p (g j i) -> p g j i", j=PACK, i=RUN),
-                in0=pairs[:, :, :, :, 0], in1=pairs[:, :, :, :, 1], op=op,
+                out=dst[:].rearrange("p (g i j) -> p g j i", i=RUN, j=PACK),
+                in0=by_run(src),
+                in1=factor[:].unsqueeze(1).unsqueeze(3).to_broadcast([P, CHUNK // RUN, PACK, RUN]),
+                op=ALU.mult,
             )
 
-        def pool_pairs(c):
-            pool(x[c][:], total[c][:], ALU.add)
-            pool(x[c][:], larger[c][:], ALU.max)
-
-        def pool_first():
-            half = CHUNK * PACK // 2
-            for h in range(2):
-                pool(x_first[h][:], total[0][:, h * half : (h + 1) * half], ALU.add)
-                pool(x_first[h][:], larger[0][:, h * half : (h + 1) * half], ALU.max)
-
         def v_on_scalar(c):
-            by_row = squared[c][:].rearrange("p (j g i) -> p j g i", j=PACK, i=RUN)
             nc.scalar.activation(
-                out=by_row.rearrange("p j g i -> p g j i"),
-                in_=total[c][:].rearrange("p (g j i) -> p g j i", j=PACK, i=RUN), func=ACT.Square,
+                out=squared[c][:].rearrange("p (j g i) -> p g j i", j=PACK, i=RUN), in_=by_run(total[c]),
+                func=ACT.Square,
             )
             for j in range(PACK):
                 nc.scalar.activation(
@@ -116,108 +114,55 @@ def tile_mix_features_pooled_over_tokens_pl_kernel(
                     scale=fv_sb[:, j : j + 1],
                 )
             nc.scalar.copy(
-                out=v_bf[c][:].rearrange("p (g i j) -> p g j i", i=4, j=PACK),
-                in_=v_rows[c][:].rearrange("p j (g i) -> p g j i", i=4),
+                out=v_bf[c][:].rearrange("p (g i j) -> p g j i", i=RUN_BF, j=PACK),
+                in_=v_rows[c][:].rearrange("p j (g i) -> p g j i", i=RUN_BF),
             )
 
-        def square(c):
-            nc.scalar.activation(out=squared[c][:], in_=total[c][:], func=ACT.Square)
-
-        def scale_and_group(dst, src, factor):
-            nc.vector.tensor_tensor(
-                out=dst[:].rearrange("p (g i j) -> p g j i", i=RUN, j=PACK),
-                in0=src[:].rearrange("p (g j i) -> p g j i", j=PACK, i=RUN),
-                in1=factor[:].unsqueeze(1).unsqueeze(3).to_broadcast([P, CHUNK // RUN, PACK, RUN]),
-                op=ALU.mult,
-            )
-
-        def scale_inputs(c):
-            scale_and_group(u_bf[c], larger[c], fa_sb)
-            scale_and_group(v_bf[c], squared[c], fv_sb)
-
-        def quantise_inputs(c):
-            nc.vector.quantize_mx(out=v_codes[c][:].bitcast(E5M2), scales=v_scales[c][:], in_=v_bf[c][:])
+        def quantise_u(c):
             nc.vector.quantize_mx(out=u_codes[c][:].bitcast(E4M3), scales=u_scales[c][:], in_=u_bf[c][:])
 
-        def pooled_passes(c, start, stop):
-            nc.tensor.matmul_mx(
-                out=acc[c][:], lhsT=v_codes[c][:].bitcast(E5M2), lhsT_scale=v_scales[c][:],
-                rhs=wb_sb[:].bitcast(E2M1), rhs_scale=planes[:, WB : WB + N], start=start, stop=False,
-            )
-            nc.tensor.matmul_mx(
-                out=acc[c][:], lhsT=u_codes[c][:].bitcast(E4M3), lhsT_scale=u_scales[c][:],
-                rhs=wa_sb[:].bitcast(E4M3), rhs_scale=planes[:, WA : WA + N], start=False, stop=stop,
-            )
+        def quantise_v(c):
+            nc.vector.quantize_mx(out=v_codes[c][:].bitcast(E5M2), scales=v_scales[c][:], in_=v_bf[c][:])
 
-        def pair_passes(c, start, stop):
-            for z in range(2):
-                at = XQ + z * B + c * CHUNK
+        def xq_passes(c):
+            for z in range(L_PASSES):
+                at = XQ_AT + z * B + c * CHUNK
                 nc.tensor.matmul_mx(
                     out=acc[c][:], lhsT=xq_sb[:, z, c * CHUNK : (c + 1) * CHUNK].bitcast(E4M3),
                     lhsT_scale=planes[:, at : at + CHUNK],
-                    rhs=wq_sb[:, z, :].bitcast(E2M1), rhs_scale=planes[:, WQ + z * N : WQ + (z + 1) * N],
-                    start=start and z == 0, stop=stop and z == 1,
+                    rhs=wq_sb[:, z, :].bitcast(E2M1), rhs_scale=planes[:, WQ_AT + z * N : WQ_AT + (z + 1) * N],
+                    start=z == 0, stop=False,
                 )
 
-        def drain(c):
-            nc.scalar.copy(out=y_t[c][:], in_=acc[c][:].rearrange("b (p r) -> b r p", r=PACK))
+        def u_pass(c):
+            nc.tensor.matmul_mx(
+                out=acc[c][:], lhsT=u_codes[c][:].bitcast(E4M3), lhsT_scale=u_scales[c][:],
+                rhs=wa_sb[:].bitcast(E4M3), rhs_scale=planes[:, WA_AT : WA_AT + N], start=False, stop=False,
+            )
 
-        def finish_last(c):
-            banks = (flipped[c], flipped[0])
-            for h in range(2):
-                rows = slice(2 * h, 2 * h + 2)
-                nc.scalar.copy(out=y_t[c][:, rows, :], in_=acc[c][:].rearrange("b (p r) -> b r p", r=PACK)[:, rows, :])
-            for h in range(2):
-                for r in range(2):
-                    nc.tensor.transpose(banks[h][:, r, :], y_t[c][:, 2 * h + r, :], ident[:])
-            nc.vector.tensor_copy(out=y[c][:, 0:2, :], in_=banks[0][:, 0:2, :])
-            nc.scalar.copy(out=y[c][:, 2:4, :], in_=banks[1][:, 0:2, :])
-            cols = out_0[:, c * CHUNK : (c + 1) * CHUNK]
-            nc.sync.dma_start(out=cols.rearrange("(p r) b -> p r b", r=PACK), in_=y[c][:])
+        def v_pass(c):
+            nc.tensor.matmul_mx(
+                out=acc[c][:], lhsT=v_codes[c][:].bitcast(E5M2), lhsT_scale=v_scales[c][:],
+                rhs=wb_sb[:].bitcast(E2M1), rhs_scale=planes[:, WB_AT : WB_AT + N], start=False, stop=True,
+            )
 
-        def drain_half(c, h):
-            rows = slice(2 * h, 2 * h + 2)
+        def drain(c, rows):
             nc.scalar.copy(out=y_t[c][:, rows, :], in_=acc[c][:].rearrange("b (p r) -> b r p", r=PACK)[:, rows, :])
 
-        def flip_half(c, h):
-            for r in range(2):
-                nc.tensor.transpose((flipped[c], flipped[0])[h][:, r, :], y_t[c][:, 2 * h + r, :], ident[:])
+        def flip(c, rows, bank):
+            for slot, r in enumerate(range(rows.start, rows.stop)):
+                nc.tensor.transpose(bank[:, slot, :], y_t[c][:, r, :], ident[:])
 
-        def store_pair(h):
+        def store_two(h):
             cols = out_0[:, 2 * h * CHUNK : 2 * (h + 1) * CHUNK]
-            nc.sync.dma_start(out=cols.rearrange("(p r) b -> p r b", r=PACK), in_=y_pair[h][:])
+            nc.sync.dma_start(out=cols.rearrange("(p r) b -> p r b", r=PACK), in_=y_two[h][:])
 
-        def store_out(c):
-            cols = out_0[:, c * CHUNK : (c + 1) * CHUNK]
-            nc.sync.dma_start(out=cols.rearrange("(p r) b -> p r b", r=PACK), in_=y[c][:])
-
-        def flip(c):
-            for r in range(PACK):
-                nc.tensor.transpose(flipped[c][:, r, :], y_t[c][:, r, :], ident[:])
-
-        def grouped_y(c):
-            return y_bf[:, c * CHUNK * PACK : (c + 1) * CHUNK * PACK]
-
-        def round_from_psum(c):
-            nc.scalar.copy(
-                out=grouped_y(c).rearrange("p (b r) -> p b r", r=PACK), in_=flipped[c][:].rearrange("p r b -> p b r")
-            )
-
-        def round_from_sbuf(c):
+        def round_y(c):
+            dst = y_bf[:, c * CHUNK * PACK : (c + 1) * CHUNK * PACK]
             nc.vector.tensor_copy(
-                out=grouped_y(c).rearrange("p (g i r) -> p g r i", i=2, r=PACK),
-                in_=y[c][:].rearrange("p r (g i) -> p g r i", i=2),
+                out=dst.rearrange("p (g i r) -> p g r i", i=RUN, r=PACK),
+                in_=y[c].rearrange("p r (g i) -> p g r i", i=RUN),
             )
-
-        def store_y(c):
-            nc.scalar.copy(out=y[c][:], in_=flipped[c][:])
-            cols = out_0[:, c * CHUNK : (c + 1) * CHUNK]
-            nc.sync.dma_start(out=cols.rearrange("(p r) b -> p r b", r=PACK), in_=y[c][:])
-
-        def store_y_vector(c):
-            nc.vector.tensor_copy(out=y[c][:], in_=flipped[c][:])
-            cols = out_0[:, c * CHUNK : (c + 1) * CHUNK]
-            nc.sync.dma_start(out=cols.rearrange("(p r) b -> p r b", r=PACK), in_=y[c][:])
 
         def quantise_y(first, count):
             lo, hi = first * CHUNK, (first + count) * CHUNK
@@ -225,102 +170,87 @@ def tile_mix_features_pooled_over_tokens_pl_kernel(
                 out=y_codes[:, lo:hi].bitcast(E4M3), scales=y_scales[:, lo:hi], in_=y_bf[:, lo * PACK : hi * PACK]
             )
 
-        def store_codes(lo, hi):
+        def store_codes(h):
+            cols = slice(2 * h * CHUNK, 2 * (h + 1) * CHUNK)
             dst = out_1[0].rearrange("p b r -> p (b r)").bitcast(I32)
-            nc.sync.dma_start(out=dst[:, lo:hi], in_=y_codes[:, lo:hi].bitcast(I32))
-
-        def load_words(dst, src):
-            nc.sync.dma_start(out=dst.bitcast(I32), in_=src.bitcast(I32))
+            nc.sync.dma_start(out=dst[:, cols], in_=y_codes[:, cols].bitcast(I32))
 
         nc.vector.memset(planes[:].bitcast(I32), 0)
         nc.vector.memset(warm[:], 0.0)
         nc.scalar.activation(out=warm[:], in_=warm[:], func=ACT.Square)
         make_identity(nc, ident[:])
-        load_scales(nc.gpsimd, WQ, wq_scales, 0)
-        load_scales(nc.gpsimd, WQ, wq_scales, 1)
-        load_scales(nc.gpsimd, WQ, wq_scales, 2)
-        load_scales(nc.gpsimd, WQ, wq_scales, 3)
 
+        load_scales(nc.gpsimd, WA_AT, wa_scales)
         load_x(0)
         nc.sync.dma_start(out=fb_sb[:], in_=fb.rearrange("(p j) o -> p (j o)", j=PACK))
         nc.sync.dma_start(out=fa_sb[:], in_=fa.rearrange("(p j) o -> p (j o)", j=PACK))
-        load_scales(nc.sync, XQ, xq_scales, 0)
-        load_scales(nc.sync, XQ, xq_scales, 1)
         load_x(1)
         load_words(xq_sb[:], xq_words.rearrange("z p n t -> p z (n t)"))
+        load_scales(nc.sync, XQ_AT, xq_scales)
         load_x(2)
-        load_scales(nc.sync, XQ, xq_scales, 2)
-        load_scales(nc.sync, XQ, xq_scales, 3)
-        load_scales(nc.sync, WB, wb_scales, 0)
-        load_scales(nc.sync, WB, wb_scales, 1)
         load_words(wq_sb[:], wq_words.rearrange("z p n -> p z n"))
-        load_words(wb_sb[:], wb_words[0])
+        load_scales(nc.sync, WQ_AT, wq_scales)
         load_x(3)
         load_words(wa_sb[:], wa_words[0].rearrange("p n t -> p (n t)"))
-        load_scales(nc.sync, WB, wb_scales, 2)
-        load_scales(nc.sync, WB, wb_scales, 3)
-        load_scales(nc.sync, WA, wa_scales, 0)
-        load_scales(nc.sync, WA, wa_scales, 1)
-        load_scales(nc.sync, WA, wa_scales, 2)
-        load_scales(nc.sync, WA, wa_scales, 3)
+        load_words(wb_sb[:], wb_words[0])
+        load_scales(nc.sync, WB_AT, wb_scales)
 
         nc.scalar.mul(out=fv_sb[:], in_=fb_sb[:], mul=0.3)
 
-        pool(x[0][:], total[0][:], ALU.add)
-        v_on_scalar(0)
-        pool(x[0][:], larger[0][:], ALU.max)
-        scale_and_group(u_bf[0], larger[0], fa_sb)
-        pool(x[1][:], total[1][:], ALU.add)
-        v_on_scalar(1)
-        pool(x[1][:], larger[1][:], ALU.max)
-        scale_and_group(u_bf[1], larger[1], fa_sb)
-        quantise_inputs(0)
-        pool(x[2][:], total[2][:], ALU.add)
-        square(2)
-        pool(x[2][:], larger[2][:], ALU.max)
-        quantise_inputs(1)
-        scale_and_group(u_bf[2], larger[2], fa_sb)
-        scale_and_group(v_bf[2], squared[2], fv_sb)
-        pair_passes(0, True, False)
-        pair_passes(1, True, False)
-        pair_passes(2, True, False)
-        pool(x[3][:], total[3][:], ALU.add)
-        square(3)
-        pooled_passes(0, False, True)
-        pooled_passes(1, False, True)
-        drain(0)
-        quantise_inputs(2)
-        pool(x[3][:], larger[3][:], ALU.max)
-        scale_and_group(v_bf[3], squared[3], fv_sb)
-        scale_and_group(u_bf[3], larger[3], fa_sb)
-        quantise_inputs(3)
-        drain(1)
-        pair_passes(3, True, False)
-        pooled_passes(2, False, True)
-        flip(0)
-        flip(1)
-        drain(2)
-        nc.scalar.copy(out=y[0][:], in_=flipped[0][:])
-        pooled_passes(3, False, True)
-        flip(2)
-        nc.vector.tensor_copy(out=y[1][:], in_=flipped[1][:])
-        store_pair(0)
-        drain_half(3, 0)
-        drain_half(3, 1)
-        round_from_sbuf(0)
-        round_from_sbuf(1)
+        for c in range(CHUNKS):
+            pool_pairs(c, total[c], ALU.add)
+            if c == 1:
+                scale_on_vector(u_bf[0], larger[0], fa_sb)
+            if c < LAST:
+                v_on_scalar(c)
+            else:
+                nc.scalar.activation(out=squared[c][:], in_=total[c][:], func=ACT.Square)
+            pool_pairs(c, larger[c], ALU.max)
+            if c > 0:
+                quantise_v(c - 1)
+                quantise_u(c - 1)
+                scale_on_vector(u_bf[c], larger[c], fa_sb)
+        scale_on_vector(v_bf[LAST], squared[LAST], fv_sb)
+        quantise_u(LAST)
+        quantise_v(LAST)
+
+        all_rows, low_rows, high_rows = slice(0, PACK), slice(0, PACK // 2), slice(PACK // 2, PACK)
+        for c in range(LAST):
+            xq_passes(c)
+        for one_pass in (u_pass, v_pass):
+            for c in (0, 1):
+                one_pass(c)
+        xq_passes(LAST)
+        u_pass(2)
+        v_pass(2)
+        for c in range(LAST):
+            drain(c, all_rows)
+        for c in (0, 1):
+            flip(c, all_rows, flipped[c])
+        u_pass(LAST)
+        v_pass(LAST)
+        flip(2, all_rows, flipped[2])
+
+        nc.scalar.copy(out=y[0], in_=flipped[0][:])
+        nc.vector.tensor_copy(out=y[1], in_=flipped[1][:])
+        store_two(0)
+        drain(LAST, low_rows)
+        drain(LAST, high_rows)
+        for c in (0, 1):
+            round_y(c)
         quantise_y(0, 2)
-        store_codes(0, 2 * CHUNK)
-        nc.scalar.copy(out=y[2][:], in_=flipped[2][:])
-        flip_half(3, 0)
-        flip_half(3, 1)
-        nc.vector.tensor_copy(out=y[3][:, 0:2, :], in_=flipped[3][:, 0:2, :])
-        nc.scalar.copy(out=y[3][:, 2:4, :], in_=flipped[0][:, 0:2, :])
-        store_pair(1)
-        round_from_sbuf(2)
-        round_from_sbuf(3)
-        quantise_y(2, 2)
-        store_codes(2 * CHUNK, B)
+        store_codes(0)
+        nc.scalar.copy(out=y[2], in_=flipped[2][:])
+        flip(LAST, low_rows, flipped[LAST])
+        flip(LAST, high_rows, flipped[0])
+        nc.vector.tensor_copy(out=y[LAST][:, low_rows, :], in_=flipped[LAST][:, low_rows, :])
+        nc.scalar.copy(out=y[LAST][:, high_rows, :], in_=flipped[0][:, low_rows, :])
+        store_two(1)
+        for c in (2, LAST):
+            round_y(c)
+        for c in (2, LAST):
+            quantise_y(c, 1)
+        store_codes(1)
         for q in range(QUADS):
             queue = nc.scalar if q % 2 == 0 else nc.sync
             queue.dma_start(

from contextlib import ExitStack

import concourse.mybir as mybir
from concourse.masks import make_identity

K, L, B, N = 512, 1024, 512, 512
FLOPS = 2 * N * B * (2 * K + L)

F32 = mybir.dt.float32
BF16 = mybir.dt.bfloat16
I32 = mybir.dt.int32
U32 = mybir.dt.uint32
U8 = mybir.dt.uint8
E4M3 = mybir.dt.float8_e4m3fn_x4
E5M2 = mybir.dt.float8_e5m2_x4
E2M1 = mybir.dt.float4_e2m1fn_x4
ALU = mybir.AluOpType
ACT = mybir.ActivationFunctionType

P = 128
PACK = 4
QUADS = 4
L_PASSES = L // (P * PACK)
CHUNK = 128
CHUNKS = B // CHUNK
LAST = CHUNKS - 1
MX_ALIGN = 64
RUN = 2
RUN_BF = 4
WB_AT, WA_AT, XQ_AT, WQ_AT, PLANE_COLS = 0, N, 2 * N, 4 * N, 6 * N


def tile_mix_features_pooled_over_tokens_pl_kernel(
    tc, xf, fa, fb, wa_words, wa_scales, wb_words, wb_scales, xq_words, xq_scales, wq_words, wq_scales,
    out_0, out_1, out_2,
):
    nc = tc.nc
    with ExitStack() as ctx:
        sb = ctx.enter_context(tc.tile_pool(name="sb", bufs=1))
        ps = ctx.enter_context(tc.psum_pool(name="ps", bufs=1))
        ctx.enter_context(tc.manual_schedule())

        def per_chunk(label, shape, dtype, count=CHUNKS):
            return [sb.tile(shape, dtype, name="%s%d" % (label, c), align_bytes=MX_ALIGN) for c in range(count)]

        x = per_chunk("x", [P, PACK, 2 * CHUNK], F32)
        larger = per_chunk("larger", [P, CHUNK * PACK], F32)
        total = per_chunk("total", [P, CHUNK * PACK], F32)
        squared = per_chunk("squared", [P, CHUNK * PACK], F32)
        v_rows = per_chunk("v_rows", [P, PACK, CHUNK], BF16, LAST)
        u_bf = per_chunk("u_bf", [P, CHUNK * PACK], BF16)
        v_bf = per_chunk("v_bf", [P, CHUNK * PACK], BF16)
        u_codes = per_chunk("u_codes", [P, CHUNK], U32)
        v_codes = per_chunk("v_codes", [P, CHUNK], U32)
        u_scales = per_chunk("u_scales", [P, CHUNK], U8)
        v_scales = per_chunk("v_scales", [P, CHUNK], U8)
        y_t = per_chunk("y_t", [CHUNK, PACK, P], F32)
        y_two = per_chunk("y_two", [P, PACK, 2 * CHUNK], F32, CHUNKS // 2)
        y = [y_two[c // 2][:, :, (c % 2) * CHUNK : (c % 2 + 1) * CHUNK] for c in range(CHUNKS)]
        acc = [ps.tile([CHUNK, N], F32, name="acc%d" % c) for c in range(CHUNKS)]
        flipped = [ps.tile([P, PACK, CHUNK], F32, name="flipped%d" % c) for c in range(CHUNKS)]

        y_bf = sb.tile([P, B * PACK], BF16, align_bytes=MX_ALIGN)
        y_codes = sb.tile([P, B], U32, align_bytes=MX_ALIGN)
        y_scales = sb.tile([P, B], U8, align_bytes=MX_ALIGN)
        fa_sb = sb.tile([P, PACK], F32)
        fb_sb = sb.tile([P, PACK], F32)
        fv_sb = sb.tile([P, PACK], F32)
        warm = sb.tile([P, 1], F32)
        ident = sb.tile([P, P], F32)
        wa_sb = sb.tile([P, N], U32, align_bytes=MX_ALIGN)
        wb_sb = sb.tile([P, 2 * N], U8, align_bytes=MX_ALIGN)
        xq_sb = sb.tile([P, L_PASSES, B], U32, align_bytes=MX_ALIGN)
        wq_sb = sb.tile([P, L_PASSES, 2 * N], U8, align_bytes=MX_ALIGN)
        planes = sb.tile([P, PLANE_COLS], U8, align_bytes=MX_ALIGN)

        def load_x(c):
            cols = xf[:, 2 * CHUNK * c : 2 * CHUNK * (c + 1)]
            nc.sync.dma_start(out=x[c][:], in_=cols.rearrange("(p j) t -> p j t", j=PACK))

        def load_words(dst, src):
            nc.sync.dma_start(out=dst.bitcast(I32), in_=src.bitcast(I32))

        def load_scales(queue, at, scales):
            passes = scales.shape[0]
            for q in range(QUADS):
                dst = planes[32 * q : 32 * q + 4, at : at + passes * N].bitcast(I32)
                src = scales[:, 4 * q : 4 * q + 4, :].rearrange("z r n -> r z n").bitcast(I32)
                queue.dma_start(out=dst.rearrange("r (z n) -> r z n", z=passes), in_=src)

        def by_run(tile):
            return tile[:].rearrange("p (g j i) -> p g j i", j=PACK, i=RUN)

        def pool_pairs(c, dst, op):
            pairs = x[c][:].rearrange("p j (g i e) -> p g j i e", i=RUN, e=2)
            nc.vector.tensor_tensor(out=by_run(dst), in0=pairs[:, :, :, :, 0], in1=pairs[:, :, :, :, 1], op=op)

        def scale_on_vector(dst, src, factor):
            nc.vector.tensor_tensor(
                out=dst[:].rearrange("p (g i j) -> p g j i", i=RUN, j=PACK),
                in0=by_run(src),
                in1=factor[:].unsqueeze(1).unsqueeze(3).to_broadcast([P, CHUNK // RUN, PACK, RUN]),
                op=ALU.mult,
            )

        def v_on_scalar(c):
            nc.scalar.activation(
                out=squared[c][:].rearrange("p (j g i) -> p g j i", j=PACK, i=RUN), in_=by_run(total[c]),
                func=ACT.Square,
            )
            for j in range(PACK):
                nc.scalar.activation(
                    out=v_rows[c][:, j, :], in_=squared[c][:, j * CHUNK : (j + 1) * CHUNK], func=ACT.Copy,
                    scale=fv_sb[:, j : j + 1],
                )
            nc.scalar.copy(
                out=v_bf[c][:].rearrange("p (g i j) -> p g j i", i=RUN_BF, j=PACK),
                in_=v_rows[c][:].rearrange("p j (g i) -> p g j i", i=RUN_BF),
            )

        def quantise_u(c):
            nc.vector.quantize_mx(out=u_codes[c][:].bitcast(E4M3), scales=u_scales[c][:], in_=u_bf[c][:])

        def quantise_v(c):
            nc.vector.quantize_mx(out=v_codes[c][:].bitcast(E5M2), scales=v_scales[c][:], in_=v_bf[c][:])

        def xq_passes(c):
            for z in range(L_PASSES):
                at = XQ_AT + z * B + c * CHUNK
                nc.tensor.matmul_mx(
                    out=acc[c][:], lhsT=xq_sb[:, z, c * CHUNK : (c + 1) * CHUNK].bitcast(E4M3),
                    lhsT_scale=planes[:, at : at + CHUNK],
                    rhs=wq_sb[:, z, :].bitcast(E2M1), rhs_scale=planes[:, WQ_AT + z * N : WQ_AT + (z + 1) * N],
                    start=z == 0, stop=False,
                )

        def u_pass(c):
            nc.tensor.matmul_mx(
                out=acc[c][:], lhsT=u_codes[c][:].bitcast(E4M3), lhsT_scale=u_scales[c][:],
                rhs=wa_sb[:].bitcast(E4M3), rhs_scale=planes[:, WA_AT : WA_AT + N], start=False, stop=False,
            )

        def v_pass(c):
            nc.tensor.matmul_mx(
                out=acc[c][:], lhsT=v_codes[c][:].bitcast(E5M2), lhsT_scale=v_scales[c][:],
                rhs=wb_sb[:].bitcast(E2M1), rhs_scale=planes[:, WB_AT : WB_AT + N], start=False, stop=True,
            )

        def drain(c, rows):
            nc.scalar.copy(out=y_t[c][:, rows, :], in_=acc[c][:].rearrange("b (p r) -> b r p", r=PACK)[:, rows, :])

        def flip(c, rows, bank):
            for slot, r in enumerate(range(rows.start, rows.stop)):
                nc.tensor.transpose(bank[:, slot, :], y_t[c][:, r, :], ident[:])

        def store_two(h):
            cols = out_0[:, 2 * h * CHUNK : 2 * (h + 1) * CHUNK]
            nc.sync.dma_start(out=cols.rearrange("(p r) b -> p r b", r=PACK), in_=y_two[h][:])

        def round_y(c):
            dst = y_bf[:, c * CHUNK * PACK : (c + 1) * CHUNK * PACK]
            nc.vector.tensor_copy(
                out=dst.rearrange("p (g i r) -> p g r i", i=RUN, r=PACK),
                in_=y[c].rearrange("p r (g i) -> p g r i", i=RUN),
            )

        def quantise_y(first, count):
            lo, hi = first * CHUNK, (first + count) * CHUNK
            nc.vector.quantize_mx(
                out=y_codes[:, lo:hi].bitcast(E4M3), scales=y_scales[:, lo:hi], in_=y_bf[:, lo * PACK : hi * PACK]
            )

        def store_codes(h):
            cols = slice(2 * h * CHUNK, 2 * (h + 1) * CHUNK)
            dst = out_1[0].rearrange("p b r -> p (b r)").bitcast(I32)
            nc.sync.dma_start(out=dst[:, cols], in_=y_codes[:, cols].bitcast(I32))

        nc.vector.memset(planes[:].bitcast(I32), 0)
        nc.vector.memset(warm[:], 0.0)
        nc.scalar.activation(out=warm[:], in_=warm[:], func=ACT.Square)
        make_identity(nc, ident[:])

        load_scales(nc.gpsimd, WA_AT, wa_scales)
        load_x(0)
        nc.sync.dma_start(out=fb_sb[:], in_=fb.rearrange("(p j) o -> p (j o)", j=PACK))
        nc.sync.dma_start(out=fa_sb[:], in_=fa.rearrange("(p j) o -> p (j o)", j=PACK))
        load_x(1)
        load_words(xq_sb[:], xq_words.rearrange("z p n t -> p z (n t)"))
        load_scales(nc.sync, XQ_AT, xq_scales)
        load_x(2)
        load_words(wq_sb[:], wq_words.rearrange("z p n -> p z n"))
        load_scales(nc.sync, WQ_AT, wq_scales)
        load_x(3)
        load_words(wa_sb[:], wa_words[0].rearrange("p n t -> p (n t)"))
        load_words(wb_sb[:], wb_words[0])
        load_scales(nc.sync, WB_AT, wb_scales)

        nc.scalar.mul(out=fv_sb[:], in_=fb_sb[:], mul=0.3)

        for c in range(CHUNKS):
            pool_pairs(c, total[c], ALU.add)
            if c == 1:
                scale_on_vector(u_bf[0], larger[0], fa_sb)
            if c < LAST:
                v_on_scalar(c)
            else:
                nc.scalar.activation(out=squared[c][:], in_=total[c][:], func=ACT.Square)
            pool_pairs(c, larger[c], ALU.max)
            if c > 0:
                quantise_v(c - 1)
                quantise_u(c - 1)
                scale_on_vector(u_bf[c], larger[c], fa_sb)
        scale_on_vector(v_bf[LAST], squared[LAST], fv_sb)
        quantise_u(LAST)
        quantise_v(LAST)

        all_rows, low_rows, high_rows = slice(0, PACK), slice(0, PACK // 2), slice(PACK // 2, PACK)
        for c in range(LAST):
            xq_passes(c)
        for one_pass in (u_pass, v_pass):
            for c in (0, 1):
                one_pass(c)
        xq_passes(LAST)
        u_pass(2)
        v_pass(2)
        for c in range(LAST):
            drain(c, all_rows)
        for c in (0, 1):
            flip(c, all_rows, flipped[c])
        u_pass(LAST)
        v_pass(LAST)
        flip(2, all_rows, flipped[2])

        nc.scalar.copy(out=y[0], in_=flipped[0][:])
        nc.vector.tensor_copy(out=y[1], in_=flipped[1][:])
        store_two(0)
        drain(LAST, low_rows)
        drain(LAST, high_rows)
        for c in (0, 1):
            round_y(c)
        quantise_y(0, 2)
        store_codes(0)
        nc.scalar.copy(out=y[2], in_=flipped[2][:])
        flip(LAST, low_rows, flipped[LAST])
        flip(LAST, high_rows, flipped[0])
        nc.vector.tensor_copy(out=y[LAST][:, low_rows, :], in_=flipped[LAST][:, low_rows, :])
        nc.scalar.copy(out=y[LAST][:, high_rows, :], in_=flipped[0][:, low_rows, :])
        store_two(1)
        for c in (2, LAST):
            round_y(c)
        for c in (2, LAST):
            quantise_y(c, 1)
        store_codes(1)
        for q in range(QUADS):
            queue = nc.scalar if q % 2 == 0 else nc.sync
            queue.dma_start(
                out=out_2[0, 4 * q : 4 * q + 4, :].bitcast(I32), in_=y_scales[32 * q : 32 * q + 4, :].bitcast(I32)
            )
